import numpy as np
import ml_dtypes


def mxq(x, axis, fmt="e4m3"):
    dtype, down = {"e4m3": (ml_dtypes.float8_e4m3fn, 7), "e5m2": (ml_dtypes.float8_e5m2, 14)}[fmt]
    v = np.moveaxis(np.asarray(x, np.float32).astype(ml_dtypes.bfloat16).astype(np.float64), axis, -1)
    blocks = v.reshape(v.shape[:-1] + (-1, 32))
    amax = np.abs(blocks).max(-1, keepdims=True)
    byte = np.maximum(np.where(amax > 0, np.frexp(amax)[1] - 1 + 127, 0) - down, 1)
    scale = np.exp2(byte - 127.0)
    codes = (blocks / scale).astype(np.float32).astype(dtype).astype(np.float64)
    return np.moveaxis((codes * scale).reshape(v.shape), -1, axis)


WIDE = False


def mx_kscale(k):
    if not WIDE:
        return np.ones(k)
    levels = np.array([10, -10, 5, -5, 0])
    if k % 512:
        return np.exp2(np.random.permutation(np.resize(levels, k // 32))).repeat(32)
    a = np.empty((k // 512, 16))
    for p in range(k // 512):
        a[p, :8] = np.random.permutation(np.resize(levels, 8))
        for g in range(8):
            far = levels[np.abs(levels - a[p, g]) >= 10]
            a[p, g + 8] = far[np.random.randint(len(far))]
    return np.exp2(a.ravel()).repeat(32)


def f64(x):
    return np.asarray(x).astype(np.float64)


def striped8(idx):
    return np.asarray(idx).reshape(8, -1, 16).transpose(0, 2, 1).reshape(128, -1).astype(np.uint16)


def unstriped8(offs):
    return offs.reshape(8, 16, -1).transpose(0, 2, 1).reshape(8, -1).astype(np.int64)


def pick8(x, idx, run):
    r = np.arange(len(x))
    return x[r[:, None], idx[r % (8 * run) // run]]


E2M1 = np.array([0.0, 0.5, 1.0, 1.5, 2.0, 3.0, 4.0, 6.0, -0.0, -0.5, -1.0, -1.5, -2.0, -3.0, -4.0, -6.0])


def pack_weight(w, fmt):
    k, n = w.shape
    w = f64(np.asarray(w, np.float32).astype(ml_dtypes.bfloat16)).reshape(k // 32, 32, n)
    amax = np.abs(w).max(1)
    if fmt == "e4m3":
        byte = np.frexp(amax)[1] - 1 + 127 - 7
    else:
        mant, ex = np.frexp(amax / 6.0)
        byte = np.where(mant > 0.5, ex, ex - 1) + 127
    byte = np.clip(np.where(amax > 0, byte, 1), 1, 254)
    scaled = (w * np.exp2(127.0 - byte)[:, None, :]).reshape(k, n).astype(np.float32)
    by_word = np.ascontiguousarray(scaled.reshape(k // 512, 128, 4, n).transpose(0, 1, 3, 2))
    if fmt == "e4m3":
        words = by_word.astype(ml_dtypes.float8_e4m3fn).view(np.uint8)
    else:
        c = by_word.astype(ml_dtypes.float4_e2m1fn).view(np.uint8) & 0xF
        words = (c[..., 0::2] | (c[..., 1::2] << 4)).reshape(k // 512, 128, 2 * n)
    return np.ascontiguousarray(words), np.ascontiguousarray(byte.astype(np.uint8).reshape(k // 512, 16, n))


def unpack_weight(words, scales, fmt):
    g, _, n = scales.shape
    words = np.ascontiguousarray(words).reshape(g, 128, n, -1)
    if fmt == "e4m3":
        vals = words.view(ml_dtypes.float8_e4m3fn).astype(np.float64)
    else:
        nib = np.empty((g, 128, n, 4), np.uint8)
        nib[..., 0::2] = words & 0xF
        nib[..., 1::2] = words >> 4
        vals = E2M1[nib]
    vals = vals * np.repeat(np.exp2(scales.astype(np.float64) - 127.0), 8, axis=1)[..., None]
    return vals.transpose(0, 1, 3, 2).reshape(g * 512, n)


D, T, I, Q = 512, 1024, 512, 128


def setup_inputs():
    n = np.random.standard_normal
    idx = np.stack([np.random.permutation(T)[:I] for _ in range(8)])
    idx2 = np.stack([np.random.permutation(T)[:I] for _ in range(8)])
    idx3 = np.stack([np.random.permutation(T)[:I] for _ in range(8)])
    idx4 = np.stack([np.random.permutation(T)[:I] for _ in range(8)])
    fd = mx_kscale(D)
    keysp = pack_weight(n((D, T)) / fd[:, None], "e2m1")
    return {
        "query": (n((D, Q)) * 1.0 / np.sqrt(D) * fd[:, None]).astype(np.float32),
        "keys_words": keysp[0],
        "keys_scales": keysp[1],
        "old": (1.0 * n((Q, T))).astype(np.float32),
        "offs": striped8(idx),
        "offs2": striped8(idx2),
        "offs3": striped8(idx3),
        "offs4": striped8(idx4),
    }


def reference(query, keys_words, keys_scales, old, offs, offs2, offs3, offs4):
    idx = unstriped8(offs)
    idx2 = unstriped8(offs2)
    idx3 = unstriped8(offs3)
    idx4 = unstriped8(offs4)
    keysu = unpack_weight(keys_words, keys_scales, "e2m1")
    queryq = mxq(f64(query), 0, "e4m3")
    a = queryq.T @ keysu
    w = pick8(a, idx, 16) - pick8(a, idx2, 16)
    f1 = np.zeros((Q, T))
    f1[np.arange(Q)[:, None], idx[np.arange(Q) % 128 // 16]] = w
    f2 = f1 + f64(old)
    y = np.maximum(pick8(f2, idx3, 16), pick8(f2, idx4, 16))
    return y

@@ -1,0 +1,115 @@
+from contextlib import ExitStack
+
+import concourse.mybir as mybir
+
+D, T, I, Q = 512, 1024, 512, 128
+FLOPS = 2 * D * Q * T
+
+F32 = mybir.dt.float32
+BF16 = mybir.dt.bfloat16
+I32 = mybir.dt.int32
+U32 = mybir.dt.uint32
+U16 = mybir.dt.uint16
+U8 = mybir.dt.uint8
+FP8X4 = mybir.dt.float8_e4m3fn_x4
+FP4X4 = mybir.dt.float4_e2m1fn_x4
+ADD = mybir.AluOpType.add
+MAX = mybir.AluOpType.max
+COPY = mybir.ActivationFunctionType.Copy
+
+P = 128
+PACK = 4
+HALF = I // 2
+LIST_COLS = I // 16
+PIECES = [256, 256, 256, 128, 128]
+
+
+def tile_attend_difference_lean_throughtwo_heads_kernel(tc, query, keys_words, keys_scales, old, offs, offs2, offs3, offs4, out):
+    nc = tc.nc
+    with ExitStack() as ctx:
+        lists = ctx.enter_context(tc.tile_pool(name="lists", bufs=1))
+        sb = ctx.enter_context(tc.tile_pool(name="sb", bufs=1))
+        psum = ctx.enter_context(tc.psum_pool(name="psum", bufs=1))
+
+        k_scales = sb.tile([P, T], U8, name="k_scales", align_bytes=64)
+        nc.vector.memset(k_scales[:].bitcast(I32), 0)
+
+        q_raw = sb.tile([P, PACK, Q], F32, name="q_raw", tag="q_then_old")
+        nc.sync.dma_start(q_raw[:], query.rearrange("(p j) q -> p j q", j=PACK))
+        k_words = sb.tile([P, 2 * T], U8, name="k_words", align_bytes=64)
+        nc.sync.dma_start(k_words[:].bitcast(I32), keys_words[0].bitcast(I32))
+        for quad in range(4):
+            queue = nc.scalar
+            queue.dma_start(k_scales[32 * quad : 32 * quad + 4, :].bitcast(I32), keys_scales[0, 4 * quad : 4 * quad + 4, :].bitcast(I32))
+
+        idx = lists.tile([P, LIST_COLS], U16, name="idx")
+        idx2 = lists.tile([P, LIST_COLS], U16, name="idx2")
+        idx3 = lists.tile([P, LIST_COLS], U16, name="idx3")
+        idx4 = lists.tile([P, LIST_COLS], U16, name="idx4")
+        nc.sync.dma_start(idx[:], offs)
+        nc.sync.dma_start(idx2[:], offs2)
+
+        f1 = sb.tile([P, T], F32, name="f1")
+        nc.vector.memset(f1[:], 0.0)
+
+        q_bf = sb.tile([P, Q, PACK], BF16, name="q_bf", align_bytes=64)
+        q_codes = sb.tile([P, Q], U32, name="q_codes", align_bytes=64)
+        q_scales = sb.tile([P, Q], U8, name="q_scales", align_bytes=64)
+        for h in range(2):
+            cols = slice(h * Q // 2, (h + 1) * Q // 2)
+            nc.vector.tensor_copy(
+                q_bf[:, cols, :].rearrange("p (c i) j -> p c j i", i=4),
+                q_raw[:, :, cols].rearrange("p j (c i) -> p c j i", i=4),
+            )
+        for h in range(2):
+            cols = slice(h * Q // 2, (h + 1) * Q // 2)
+            nc.vector.quantize_mx(out=q_codes[:, cols].bitcast(FP8X4), scales=q_scales[:, cols], in_=q_bf[:, cols, :].rearrange("p q j -> p (q j)"))
+
+        old_sb = sb.tile([P, T], F32, name="old_sb", tag="q_then_old")
+        nc.sync.dma_start(old_sb[:], old)
+        nc.sync.dma_start(idx3[:], offs3)
+        nc.sync.dma_start(idx4[:], offs4)
+
+        a = sb.tile([P, T], F32, name="a")
+        t0 = 0
+        for n, width in enumerate(PIECES):
+            bank = psum.tile([P, width], F32, name="bank%d" % n)
+            nc.tensor.matmul_mx(
+                out=bank[:],
+                lhsT=q_codes[:].bitcast(FP8X4),
+                lhsT_scale=q_scales[:],
+                rhs=k_words[:, 2 * t0 : 2 * (t0 + width)].bitcast(FP4X4),
+                rhs_scale=k_scales[:, t0 : t0 + width],
+                start=True,
+                stop=True,
+            )
+            if n % 2 == 0:
+                nc.vector.tensor_copy(a[:, t0 : t0 + width], bank[:])
+            else:
+                nc.scalar.copy(a[:, t0 : t0 + width], bank[:])
+            t0 = t0 + width
+
+        def half(tile, h):
+            return tile[:, h * LIST_COLS // 2 : (h + 1) * LIST_COLS // 2]
+
+        for h in range(2):
+            plus = sb.tile([P, HALF], F32, name="plus%d" % h)
+            minus = sb.tile([P, HALF], F32, name="minus%d" % h)
+            nc.scalar.activation(minus[:], a[:].indirect(half(idx2, h)), COPY, scale=-1.0)
+            if h == 0:
+                nc.vector.tensor_copy(plus[:], a[:].indirect(half(idx, h)))
+            else:
+                nc.scalar.activation(plus[:], a[:].indirect(half(idx, h)), COPY)
+            nc.vector.tensor_tensor(f1[:].indirect(half(idx, h)), plus[:], minus[:], ADD)
+
+        f2 = sb.tile([P, T], F32, name="f2")
+        nc.vector.tensor_tensor(f2[:], f1[:], old_sb[:], ADD)
+
+        for h in range(2):
+            g3 = sb.tile([P, HALF], F32, name="g3_%d" % h)
+            g4 = sb.tile([P, HALF], F32, name="g4_%d" % h)
+            res = sb.tile([P, HALF], F32, name="res%d" % h)
+            nc.vector.tensor_copy(g3[:], f2[:].indirect(half(idx3, h)))
+            nc.scalar.activation(g4[:], f2[:].indirect(half(idx4, h)), COPY)
+            nc.vector.tensor_tensor(res[:], g3[:], g4[:], MAX)
+            nc.sync.dma_start(out[:, h * HALF : (h + 1) * HALF], res[:])

@@ -32,7 +32,6 @@ def tile_attend_difference_lean_throughtwo_heads_kernel(tc, query, keys_words, k
         psum = ctx.enter_context(tc.psum_pool(name="psum", bufs=1))
 
         k_scales = sb.tile([P, T], U8, name="k_scales", align_bytes=64)
-        nc.vector.memset(k_scales[:].bitcast(I32), 0)
 
         q_raw = sb.tile([P, PACK, Q], F32, name="q_raw", tag="q_then_old")
         nc.sync.dma_start(q_raw[:], query.rearrange("(p j) q -> p j q", j=PACK))

@@ -22,6 +22,7 @@ PACK = 4
 HALF = I // 2
 LIST_COLS = I // 16
 PIECES = [256, 256, 256, 128, 128]
+OUT_PIECES = [256, 128, 128]
 
 
 def tile_attend_difference_lean_throughtwo_heads_kernel(tc, query, keys_words, keys_scales, old, offs, offs2, offs3, offs4, out):
@@ -104,11 +105,17 @@ def tile_attend_difference_lean_throughtwo_heads_kernel(tc, query, keys_words, k
         f2 = sb.tile([P, T], F32, name="f2")
         nc.vector.tensor_tensor(f2[:], f1[:], old_sb[:], ADD)
 
+        g3 = []
+        g4 = []
         for h in range(2):
-            g3 = sb.tile([P, HALF], F32, name="g3_%d" % h)
-            g4 = sb.tile([P, HALF], F32, name="g4_%d" % h)
-            res = sb.tile([P, HALF], F32, name="res%d" % h)
-            nc.vector.tensor_copy(g3[:], f2[:].indirect(half(idx3, h)))
-            nc.scalar.activation(g4[:], f2[:].indirect(half(idx4, h)), COPY)
-            nc.vector.tensor_tensor(res[:], g3[:], g4[:], MAX)
-            nc.sync.dma_start(out[:, h * HALF : (h + 1) * HALF], res[:])
+            g3.append(sb.tile([P, HALF], F32, name="g3_%d" % h))
+            g4.append(sb.tile([P, HALF], F32, name="g4_%d" % h))
+            nc.vector.tensor_copy(g3[h][:], f2[:].indirect(half(idx3, h)))
+            nc.scalar.activation(g4[h][:], f2[:].indirect(half(idx4, h)), COPY)
+        i0 = 0
+        for n, width in enumerate(OUT_PIECES):
+            res = sb.tile([P, width], F32, name="res%d" % n)
+            h, c0 = divmod(i0, HALF)
+            nc.vector.tensor_tensor(res[:], g3[h][:, c0 : c0 + width], g4[h][:, c0 : c0 + width], MAX)
+            nc.sync.dma_start(out[:, i0 : i0 + width], res[:])
+            i0 = i0 + width

from contextlib import ExitStack

import concourse.mybir as mybir

D, T, I, Q = 512, 1024, 512, 128
FLOPS = 2 * D * Q * T

F32 = mybir.dt.float32
BF16 = mybir.dt.bfloat16
I32 = mybir.dt.int32
U32 = mybir.dt.uint32
U16 = mybir.dt.uint16
U8 = mybir.dt.uint8
FP8X4 = mybir.dt.float8_e4m3fn_x4
FP4X4 = mybir.dt.float4_e2m1fn_x4
ADD = mybir.AluOpType.add
MAX = mybir.AluOpType.max
COPY = mybir.ActivationFunctionType.Copy

P = 128
PACK = 4
HALF = I // 2
LIST_COLS = I // 16
PIECES = [256, 256, 256, 128, 128]
OUT_PIECES = [256, 128, 128]


def tile_attend_difference_lean_throughtwo_heads_kernel(tc, query, keys_words, keys_scales, old, offs, offs2, offs3, offs4, out):
    nc = tc.nc
    with ExitStack() as ctx:
        lists = ctx.enter_context(tc.tile_pool(name="lists", bufs=1))
        sb = ctx.enter_context(tc.tile_pool(name="sb", bufs=1))
        psum = ctx.enter_context(tc.psum_pool(name="psum", bufs=1))

        k_scales = sb.tile([P, T], U8, name="k_scales", align_bytes=64)

        q_raw = sb.tile([P, PACK, Q], F32, name="q_raw", tag="q_then_old")
        nc.sync.dma_start(q_raw[:], query.rearrange("(p j) q -> p j q", j=PACK))
        k_words = sb.tile([P, 2 * T], U8, name="k_words", align_bytes=64)
        nc.sync.dma_start(k_words[:].bitcast(I32), keys_words[0].bitcast(I32))
        for quad in range(4):
            queue = nc.scalar
            queue.dma_start(k_scales[32 * quad : 32 * quad + 4, :].bitcast(I32), keys_scales[0, 4 * quad : 4 * quad + 4, :].bitcast(I32))

        idx = lists.tile([P, LIST_COLS], U16, name="idx")
        idx2 = lists.tile([P, LIST_COLS], U16, name="idx2")
        idx3 = lists.tile([P, LIST_COLS], U16, name="idx3")
        idx4 = lists.tile([P, LIST_COLS], U16, name="idx4")
        nc.sync.dma_start(idx[:], offs)
        nc.sync.dma_start(idx2[:], offs2)

        f1 = sb.tile([P, T], F32, name="f1")
        nc.vector.memset(f1[:], 0.0)

        q_bf = sb.tile([P, Q, PACK], BF16, name="q_bf", align_bytes=64)
        q_codes = sb.tile([P, Q], U32, name="q_codes", align_bytes=64)
        q_scales = sb.tile([P, Q], U8, name="q_scales", align_bytes=64)
        for h in range(2):
            cols = slice(h * Q // 2, (h + 1) * Q // 2)
            nc.vector.tensor_copy(
                q_bf[:, cols, :].rearrange("p (c i) j -> p c j i", i=4),
                q_raw[:, :, cols].rearrange("p j (c i) -> p c j i", i=4),
            )
        for h in range(2):
            cols = slice(h * Q // 2, (h + 1) * Q // 2)
            nc.vector.quantize_mx(out=q_codes[:, cols].bitcast(FP8X4), scales=q_scales[:, cols], in_=q_bf[:, cols, :].rearrange("p q j -> p (q j)"))

        old_sb = sb.tile([P, T], F32, name="old_sb", tag="q_then_old")
        nc.sync.dma_start(old_sb[:], old)
        nc.sync.dma_start(idx3[:], offs3)
        nc.sync.dma_start(idx4[:], offs4)

        a = sb.tile([P, T], F32, name="a")
        t0 = 0
        for n, width in enumerate(PIECES):
            bank = psum.tile([P, width], F32, name="bank%d" % n)
            nc.tensor.matmul_mx(
                out=bank[:],
                lhsT=q_codes[:].bitcast(FP8X4),
                lhsT_scale=q_scales[:],
                rhs=k_words[:, 2 * t0 : 2 * (t0 + width)].bitcast(FP4X4),
                rhs_scale=k_scales[:, t0 : t0 + width],
                start=True,
                stop=True,
            )
            if n % 2 == 0:
                nc.vector.tensor_copy(a[:, t0 : t0 + width], bank[:])
            else:
                nc.scalar.copy(a[:, t0 : t0 + width], bank[:])
            t0 = t0 + width

        def half(tile, h):
            return tile[:, h * LIST_COLS // 2 : (h + 1) * LIST_COLS // 2]

        for h in range(2):
            plus = sb.tile([P, HALF], F32, name="plus%d" % h)
            minus = sb.tile([P, HALF], F32, name="minus%d" % h)
            nc.scalar.activation(minus[:], a[:].indirect(half(idx2, h)), COPY, scale=-1.0)
            if h == 0:
                nc.vector.tensor_copy(plus[:], a[:].indirect(half(idx, h)))
            else:
                nc.scalar.activation(plus[:], a[:].indirect(half(idx, h)), COPY)
            nc.vector.tensor_tensor(f1[:].indirect(half(idx, h)), plus[:], minus[:], ADD)

        f2 = sb.tile([P, T], F32, name="f2")
        nc.vector.tensor_tensor(f2[:], f1[:], old_sb[:], ADD)

        g3 = []
        g4 = []
        for h in range(2):
            g3.append(sb.tile([P, HALF], F32, name="g3_%d" % h))
            g4.append(sb.tile([P, HALF], F32, name="g4_%d" % h))
            nc.vector.tensor_copy(g3[h][:], f2[:].indirect(half(idx3, h)))
            nc.scalar.activation(g4[h][:], f2[:].indirect(half(idx4, h)), COPY)
        i0 = 0
        for n, width in enumerate(OUT_PIECES):
            res = sb.tile([P, width], F32, name="res%d" % n)
            h, c0 = divmod(i0, HALF)
            nc.vector.tensor_tensor(res[:], g3[h][:, c0 : c0 + width], g4[h][:, c0 : c0 + width], MAX)
            nc.sync.dma_start(out[:, i0 : i0 + width], res[:])
            i0 = i0 + width
